import numpy as np
import ml_dtypes


def mxq(x, axis, fmt="e4m3"):
    dtype, down = {"e4m3": (ml_dtypes.float8_e4m3fn, 7), "e5m2": (ml_dtypes.float8_e5m2, 14)}[fmt]
    v = np.moveaxis(np.asarray(x, np.float32).astype(ml_dtypes.bfloat16).astype(np.float64), axis, -1)
    blocks = v.reshape(v.shape[:-1] + (-1, 32))
    amax = np.abs(blocks).max(-1, keepdims=True)
    byte = np.maximum(np.where(amax > 0, np.frexp(amax)[1] - 1 + 127, 0) - down, 1)
    scale = np.exp2(byte - 127.0)
    codes = (blocks / scale).astype(np.float32).astype(dtype).astype(np.float64)
    return np.moveaxis((codes * scale).reshape(v.shape), -1, axis)


WIDE = False


def mx_kscale(k):
    if not WIDE:
        return np.ones(k)
    levels = np.array([10, -10, 5, -5, 0])
    if k % 512:
        return np.exp2(np.random.permutation(np.resize(levels, k // 32))).repeat(32)
    a = np.empty((k // 512, 16))
    for p in range(k // 512):
        a[p, :8] = np.random.permutation(np.resize(levels, 8))
        for g in range(8):
            far = levels[np.abs(levels - a[p, g]) >= 10]
            a[p, g + 8] = far[np.random.randint(len(far))]
    return np.exp2(a.ravel()).repeat(32)


def f64(x):
    return np.asarray(x).astype(np.float64)


def striped8(idx):
    return np.asarray(idx).reshape(8, -1, 16).transpose(0, 2, 1).reshape(128, -1).astype(np.uint16)


def unstriped8(offs):
    return offs.reshape(8, 16, -1).transpose(0, 2, 1).reshape(8, -1).astype(np.int64)


def pick8(x, idx, run):
    r = np.arange(len(x))
    return x[r[:, None], idx[r % (8 * run) // run]]


E2M1 = np.array([0.0, 0.5, 1.0, 1.5, 2.0, 3.0, 4.0, 6.0, -0.0, -0.5, -1.0, -1.5, -2.0, -3.0, -4.0, -6.0])


def pack_weight(w, fmt):
    k, n = w.shape
    w = f64(np.asarray(w, np.float32).astype(ml_dtypes.bfloat16)).reshape(k // 32, 32, n)
    amax = np.abs(w).max(1)
    if fmt == "e4m3":
        byte = np.frexp(amax)[1] - 1 + 127 - 7
    else:
        mant, ex = np.frexp(amax / 6.0)
        byte = np.where(mant > 0.5, ex, ex - 1) + 127
    byte = np.clip(np.where(amax > 0, byte, 1), 1, 254)
    scaled = (w * np.exp2(127.0 - byte)[:, None, :]).reshape(k, n).astype(np.float32)
    by_word = np.ascontiguousarray(scaled.reshape(k // 512, 128, 4, n).transpose(0, 1, 3, 2))
    if fmt == "e4m3":
        words = by_word.astype(ml_dtypes.float8_e4m3fn).view(np.uint8)
    else:
        c = by_word.astype(ml_dtypes.float4_e2m1fn).view(np.uint8) & 0xF
        words = (c[..., 0::2] | (c[..., 1::2] << 4)).reshape(k // 512, 128, 2 * n)
    return np.ascontiguousarray(words), np.ascontiguousarray(byte.astype(np.uint8).reshape(k // 512, 16, n))


def unpack_weight(words, scales, fmt):
    g, _, n = scales.shape
    words = np.ascontiguousarray(words).reshape(g, 128, n, -1)
    if fmt == "e4m3":
        vals = words.view(ml_dtypes.float8_e4m3fn).astype(np.float64)
    else:
        nib = np.empty((g, 128, n, 4), np.uint8)
        nib[..., 0::2] = words & 0xF
        nib[..., 1::2] = words >> 4
        vals = E2M1[nib]
    vals = vals * np.repeat(np.exp2(scales.astype(np.float64) - 127.0), 8, axis=1)[..., None]
    return vals.transpose(0, 1, 3, 2).reshape(g * 512, n)


D, T, I, Q, G = 512, 1024, 512, 128, 64


def setup_inputs():
    n = np.random.standard_normal
    idx = np.stack([np.random.permutation(T)[:I] for _ in range(8)])
    idx2 = np.stack([np.random.permutation(T)[:I] for _ in range(8)])
    idx3 = np.stack([np.random.permutation(T)[:I] for _ in range(8)])
    idx4 = np.stack([np.random.permutation(T)[:I] for _ in range(8)])
    fd = mx_kscale(D)
    keysp = pack_weight(n((D, T)) / fd[:, None], "e4m3")
    return {
        "query": (n((D, Q)) * 1.0 / np.sqrt(D) * fd[:, None]).astype(np.float32),
        "keys_words": keysp[0],
        "keys_scales": keysp[1],
        "lam": (np.random.uniform(0.4, 1.0, (Q, 1))).astype(np.float32),
        "old": (np.random.uniform(0.0, 2.0, (Q, T))).astype(np.float32),
        "gainm": (np.random.uniform(0.5, 1.5, (Q, I))).astype(np.float32),
        "offs": striped8(idx),
        "offs2": striped8(idx2),
        "offs3": striped8(idx3),
        "offs4": striped8(idx4),
    }


def reference(query, keys_words, keys_scales, lam, old, gainm, offs, offs2, offs3, offs4):
    idx = unstriped8(offs)
    idx2 = unstriped8(offs2)
    idx3 = unstriped8(offs3)
    idx4 = unstriped8(offs4)
    keysu = unpack_weight(keys_words, keys_scales, "e4m3")
    queryq = mxq(f64(query), 0, "e4m3")
    a = queryq.T @ keysu
    s = pick8(a, idx, 16) + np.tanh(pick8(a, idx2, 16) - pick8(a, idx3, 16)) * f64(lam)
    p = np.exp(s)
    pg = p.reshape(Q, G, I // G).sum(axis=2)
    z0 = np.sum(pg, axis=1, keepdims=True)
    k0 = 1.0 / (z0 - pg)
    kr = np.repeat(k0, I // G, axis=1)
    w = p * kr
    ws = w * f64(gainm) * 64.0
    wf = np.zeros((Q, T))
    wf[np.arange(Q)[:, None], idx4[np.arange(Q) % 128 // 16]] = ws
    y = f64(old) + wf
    return y

@@ -1,0 +1,220 @@
+from contextlib import ExitStack
+
+import concourse.mybir as mybir
+
+D, T, SLOTS, Q, RUN = 512, 1024, 512, 128, 8
+P = 128
+PACK = 4
+HALF = SLOTS // 2
+GROUPS = SLOTS // RUN
+KEY_LOAD = 512
+PASSES = [256,256,256,128,128]
+FIRST = 128
+STORES = [192,256,256,192,128]
+
+F32 = mybir.dt.float32
+BF16 = mybir.dt.bfloat16
+I32 = mybir.dt.int32
+U32 = mybir.dt.uint32
+U16 = mybir.dt.uint16
+U8 = mybir.dt.uint8
+FP8X4 = mybir.dt.float8_e4m3fn_x4
+ALU = mybir.AluOpType
+ACT = mybir.ActivationFunctionType
+AX = mybir.AxisListType
+
+FLOPS = 2 * D * Q * T
+
+
+def tile_attend_seconded_outside_moved_heads_kernel(
+    tc, query, keys_words, keys_scales, lam, old, gainm, offs, offs2, offs3, offs4, out
+):
+    nc = tc.nc
+    with ExitStack() as ctx:
+        lists = ctx.enter_context(tc.tile_pool(name="lists", bufs=1))
+        sb = ctx.enter_context(tc.tile_pool(name="sb", bufs=1))
+        ps = ctx.enter_context(tc.psum_pool(name="ps", bufs=1))
+
+        own_list = lists.tile([P, SLOTS // 16], U16, name="own_list")
+        second_list = lists.tile([P, SLOTS // 16], U16, name="second_list")
+        oppo_list = lists.tile([P, SLOTS // 16], U16, name="oppo_list")
+        place_list = lists.tile([P, SLOTS // 16], U16, name="place_list")
+
+        q_raw = sb.tile([P, PACK, Q], F32, name="q_raw")
+        nc.sync.dma_start(out=q_raw[:], in_=query.rearrange("(p j) q -> p j q", j=PACK))
+
+        k_scales = sb.tile([P, T], U8, name="k_scales", align_bytes=64)
+        nc.gpsimd.memset(k_scales[:].bitcast(U32), 0)
+        for quad in range(4):
+            nc.scalar.dma_start(
+                out=k_scales[32 * quad : 32 * quad + 4, :].bitcast(I32),
+                in_=keys_scales[0, 4 * quad : 4 * quad + 4, :].bitcast(I32),
+            )
+
+        words = keys_words[0].rearrange("p n t -> p (n t)")
+        k_words = []
+        for b in range(T // KEY_LOAD):
+            kw = sb.tile([P, KEY_LOAD], U32, name="k_words%d" % b, align_bytes=64)
+            nc.sync.dma_start(
+                out=kw[:].bitcast(I32),
+                in_=words[:, b * KEY_LOAD * PACK : (b + 1) * KEY_LOAD * PACK].bitcast(I32),
+            )
+            k_words.append(kw)
+
+        nc.sync.dma_start(oppo_list[:], offs3)
+        nc.sync.dma_start(own_list[:], offs)
+        nc.sync.dma_start(second_list[:], offs2)
+        lam_t = sb.tile([P, 1], F32, name="lam_t")
+        nc.sync.dma_start(out=lam_t[:], in_=lam)
+        gain_t = sb.tile([P, SLOTS], F32, name="gain_t")
+        nc.sync.dma_start(out=gain_t[:], in_=gainm)
+        nc.sync.dma_start(place_list[:], offs4)
+        old_t = sb.tile([P, T], F32, name="old_t")
+        nc.sync.dma_start(out=old_t[:], in_=old)
+
+        placed = sb.tile([P, T], F32, name="placed")
+        nc.vector.memset(placed[:], 0.0)
+
+        q_bf = sb.tile([P, Q, PACK], BF16, name="q_bf", align_bytes=64)
+        q_words = sb.tile([P, Q], U32, name="q_words", align_bytes=64)
+        q_scales = sb.tile([P, Q], U8, name="q_scales", align_bytes=64)
+        q_halves = [slice(0, Q // 2), slice(Q // 2, Q)]
+        for cols in q_halves:
+            nc.vector.tensor_copy(
+                out=q_bf[:, cols, :].rearrange("p (c i) t -> p c t i", i=4),
+                in_=q_raw[:, :, cols].rearrange("p t (c i) -> p c t i", i=4),
+            )
+        for cols in q_halves:
+            nc.vector.quantize_mx(
+                out=q_words[:, cols].bitcast(FP8X4),
+                scales=q_scales[:, cols],
+                in_=q_bf[:, cols, :].rearrange("p q t -> p (q t)"),
+            )
+
+        scores = sb.tile([P, T], F32, name="scores")
+        lo = 0
+        for b, width in enumerate(PASSES):
+            acc = ps.tile([P, width], F32, name="acc%d" % b)
+            cols = slice(lo, lo + width)
+            load, start = divmod(lo, KEY_LOAD)
+            lo = lo + width
+            nc.tensor.matmul_mx(
+                out=acc[:],
+                lhsT=q_words[:].bitcast(FP8X4),
+                lhsT_scale=q_scales[:],
+                rhs=k_words[load][:, start : start + width].bitcast(FP8X4),
+                rhs_scale=k_scales[:, cols],
+                start=True,
+                stop=True,
+            )
+            if b % 2 == 1:
+                nc.vector.tensor_copy(out=scores[:, cols], in_=acc[:])
+            else:
+                nc.scalar.activation(out=scores[:, cols], in_=acc[:], func=ACT.Copy)
+
+        halves = [slice(h * HALF, (h + 1) * HALF) for h in range(2)]
+        list_halves = [slice(h * HALF // 16, (h + 1) * HALF // 16) for h in range(2)]
+        run_halves = [slice(h * GROUPS // 2, (h + 1) * GROUPS // 2) for h in range(2)]
+
+        own = sb.tile([P, SLOTS], F32, name="own")
+        oppo = [sb.tile([P, HALF], F32, name="oppo%d" % h) for h in range(2)]
+        diff = [sb.tile([P, HALF], F32, name="diff%d" % h) for h in range(2)]
+        bend = [sb.tile([P, HALF], F32, name="bend%d" % h) for h in range(2)]
+        s_t = [sb.tile([P, HALF], F32, name="s%d" % h) for h in range(2)]
+        p_t = sb.tile([P, SLOTS], F32, name="p_t")
+        z_t = [sb.tile([P, 1], F32, name="z%d" % h) for h in range(2)]
+        pg = sb.tile([P, GROUPS], F32, name="pg")
+        den = sb.tile([P, GROUPS], F32, name="den")
+        inv = sb.tile([P, GROUPS], F32, name="inv")
+        spread = sb.tile([P, SLOTS], F32, name="spread")
+        gained = sb.tile([P, SLOTS], F32, name="gained")
+        neg_max = sb.tile([P, 1], F32, name="neg_max")
+
+        for h in range(2):
+            nc.scalar.activation(
+                out=oppo[h][:], in_=scores[:].indirect(oppo_list[:, list_halves[h]]), func=ACT.Copy
+            )
+        nc.vector.tensor_copy(out=own[:, halves[0]], in_=scores[:].indirect(own_list[:, list_halves[0]]))
+        nc.scalar.activation(
+            out=own[:, halves[1]], in_=scores[:].indirect(own_list[:, list_halves[1]]), func=ACT.Copy
+        )
+        for h in range(2):
+            nc.vector.tensor_tensor(
+                out=diff[h][:],
+                in0=scores[:].indirect(second_list[:, list_halves[h]]),
+                in1=oppo[h][:],
+                op=ALU.subtract,
+            )
+        for h in range(2):
+            nc.scalar.activation(out=bend[h][:], in_=diff[h][:], func=ACT.Tanh)
+        nc.vector.tensor_reduce(out=neg_max[:], in_=own[:], axis=AX.X, op=ALU.max, negate=True)
+        for h in range(2):
+            nc.vector.scalar_tensor_tensor(
+                out=s_t[h][:],
+                in0=bend[h][:],
+                scalar=lam_t[:],
+                in1=own[:, halves[h]],
+                op0=ALU.mult,
+                op1=ALU.add,
+            )
+        for h in range(2):
+            nc.scalar.activation(
+                out=p_t[:, halves[h]], in_=s_t[h][:], func=ACT.Exp, bias=neg_max[:], accum_out=z_t[h][:]
+            )
+        def run_sums(h):
+            nc.vector.tensor_reduce(
+                out=pg[:, run_halves[h]],
+                in_=p_t[:, halves[h]].rearrange("p (g j) -> p g j", j=RUN),
+                axis=AX.X,
+                op=ALU.add,
+            )
+
+        def times_gain(lo, hi):
+            nc.vector.tensor_tensor(
+                out=gained[:, lo:hi], in0=p_t[:, lo:hi], in1=gain_t[:, lo:hi], op=ALU.mult
+            )
+
+        def invert(lo, hi):
+            runs = slice(lo // RUN, hi // RUN)
+            nc.vector.reciprocal(out=inv[:, runs], in_=den[:, runs])
+            nc.scalar.activation(
+                out=spread[:, lo:hi].rearrange("p (g j) -> p g j", j=RUN),
+                in_=inv[:, runs].unsqueeze(2).to_broadcast([P, (hi - lo) // RUN, RUN]),
+                func=ACT.Copy,
+                scale=-64.0,
+            )
+
+        def place(lo, hi):
+            nc.vector.tensor_tensor(
+                out=placed[:].indirect(place_list[:, lo // 16 : hi // 16]),
+                in0=gained[:, lo:hi],
+                in1=spread[:, lo:hi],
+                op=ALU.mult,
+            )
+
+        run_sums(0)
+        times_gain(0, HALF)
+        run_sums(1)
+        times_gain(HALF, HALF + HALF // 2)
+        nc.vector.tensor_scalar(
+            out=den[:],
+            in0=pg[:],
+            scalar1=z_t[0][:],
+            scalar2=z_t[1][:],
+            op0=ALU.subtract,
+            op1=ALU.subtract,
+        )
+        times_gain(HALF + HALF // 2, SLOTS)
+        invert(0, FIRST)
+        invert(FIRST, SLOTS)
+        place(0, FIRST)
+        place(FIRST, SLOTS)
+
+        lo = 0
+        for c, width in enumerate(STORES):
+            cols = slice(lo, lo + width)
+            res = sb.tile([P, width], F32, name="res%d" % c)
+            nc.vector.tensor_tensor(out=res[:], in0=placed[:, cols], in1=old_t[:, cols], op=ALU.add)
+            queue = nc.sync if c % 2 == 0 else nc.scalar
+            queue.dma_start(out=out[:, cols], in_=res[:])
+            lo = lo + width

@@ -8,9 +8,10 @@ PACK = 4
 HALF = SLOTS // 2
 GROUPS = SLOTS // RUN
 KEY_LOAD = 512
+PLANE = 256
 PASSES = [256,256,256,128,128]
 FIRST = 128
-STORES = [192,256,256,192,128]
+STORES = [128,256,256,256,128]
 
 F32 = mybir.dt.float32
 BF16 = mybir.dt.bfloat16
@@ -43,12 +44,14 @@ def tile_attend_seconded_outside_moved_heads_kernel(
         q_raw = sb.tile([P, PACK, Q], F32, name="q_raw")
         nc.sync.dma_start(out=q_raw[:], in_=query.rearrange("(p j) q -> p j q", j=PACK))
 
-        k_scales = sb.tile([P, T], U8, name="k_scales", align_bytes=64)
-        nc.gpsimd.memset(k_scales[:].bitcast(U32), 0)
+        k_scales = sb.tile([P, PLANE], U8, name="k_scales", align_bytes=64)
+        nc.vector.memset(k_scales[:].bitcast(U32), 0)
         for quad in range(4):
             nc.scalar.dma_start(
-                out=k_scales[32 * quad : 32 * quad + 4, :].bitcast(I32),
-                in_=keys_scales[0, 4 * quad : 4 * quad + 4, :].bitcast(I32),
+                out=k_scales[32 * quad : 32 * quad + 16, :].bitcast(I32),
+                in_=keys_scales[0, 4 * quad : 4 * quad + 4, :]
+                .bitcast(I32)
+                .rearrange("r (v c) -> v r c", v=T // PLANE),
             )
 
         words = keys_words[0].rearrange("p n t -> p (n t)")
@@ -62,8 +65,8 @@ def tile_attend_seconded_outside_moved_heads_kernel(
             k_words.append(kw)
 
         nc.sync.dma_start(oppo_list[:], offs3)
-        nc.sync.dma_start(own_list[:], offs)
         nc.sync.dma_start(second_list[:], offs2)
+        nc.sync.dma_start(own_list[:], offs)
         lam_t = sb.tile([P, 1], F32, name="lam_t")
         nc.sync.dma_start(out=lam_t[:], in_=lam)
         gain_t = sb.tile([P, SLOTS], F32, name="gain_t")
@@ -97,13 +100,14 @@ def tile_attend_seconded_outside_moved_heads_kernel(
             acc = ps.tile([P, width], F32, name="acc%d" % b)
             cols = slice(lo, lo + width)
             load, start = divmod(lo, KEY_LOAD)
+            plane, first = divmod(lo, PLANE)
             lo = lo + width
             nc.tensor.matmul_mx(
                 out=acc[:],
                 lhsT=q_words[:].bitcast(FP8X4),
                 lhsT_scale=q_scales[:],
                 rhs=k_words[load][:, start : start + width].bitcast(FP8X4),
-                rhs_scale=k_scales[:, cols],
+                rhs_scale=k_scales[4 * plane : P, first : first + width],
                 start=True,
                 stop=True,
             )
@@ -130,14 +134,11 @@ def tile_attend_seconded_outside_moved_heads_kernel(
         gained = sb.tile([P, SLOTS], F32, name="gained")
         neg_max = sb.tile([P, 1], F32, name="neg_max")
 
-        for h in range(2):
-            nc.scalar.activation(
-                out=oppo[h][:], in_=scores[:].indirect(oppo_list[:, list_halves[h]]), func=ACT.Copy
-            )
-        nc.vector.tensor_copy(out=own[:, halves[0]], in_=scores[:].indirect(own_list[:, list_halves[0]]))
+        nc.vector.tensor_copy(out=oppo[0][:], in_=scores[:].indirect(oppo_list[:, list_halves[0]]))
         nc.scalar.activation(
-            out=own[:, halves[1]], in_=scores[:].indirect(own_list[:, list_halves[1]]), func=ACT.Copy
+            out=oppo[1][:], in_=scores[:].indirect(oppo_list[:, list_halves[1]]), func=ACT.Copy
         )
+        nc.scalar.activation(out=own[:], in_=scores[:].indirect(own_list[:]), func=ACT.Copy)
         for h in range(2):
             nc.vector.tensor_tensor(
                 out=diff[h][:],
@@ -181,7 +182,7 @@ def tile_attend_seconded_outside_moved_heads_kernel(
                 out=spread[:, lo:hi].rearrange("p (g j) -> p g j", j=RUN),
                 in_=inv[:, runs].unsqueeze(2).to_broadcast([P, (hi - lo) // RUN, RUN]),
                 func=ACT.Copy,
-                scale=-64.0,
+                scale=64.0,
             )
 
         def place(lo, hi):
@@ -192,21 +193,26 @@ def tile_attend_seconded_outside_moved_heads_kernel(
                 op=ALU.mult,
             )
 
+        def outside(h):
+            nc.scalar.activation(
+                out=den[:, run_halves[h]],
+                in_=pg[:, run_halves[h]],
+                func=ACT.Identity,
+                scale=-1.0,
+                bias=z_all[:],
+            )
+
+        z_all = sb.tile([P, 1], F32, name="z_all")
+        nc.scalar.activation(out=z_all[:], in_=z_t[0][:], func=ACT.Identity, bias=z_t[1][:])
         run_sums(0)
-        times_gain(0, HALF)
         run_sums(1)
-        times_gain(HALF, HALF + HALF // 2)
-        nc.vector.tensor_scalar(
-            out=den[:],
-            in0=pg[:],
-            scalar1=z_t[0][:],
-            scalar2=z_t[1][:],
-            op0=ALU.subtract,
-            op1=ALU.subtract,
-        )
-        times_gain(HALF + HALF // 2, SLOTS)
+        outside(0)
+        outside(1)
+        times_gain(0, HALF)
+        times_gain(HALF, SLOTS - FIRST)
         invert(0, FIRST)
         invert(FIRST, SLOTS)
+        times_gain(SLOTS - FIRST, SLOTS)
         place(0, FIRST)
         place(FIRST, SLOTS)
 

@@ -44,10 +44,12 @@ def tile_attend_seconded_outside_moved_heads_kernel(
         q_raw = sb.tile([P, PACK, Q], F32, name="q_raw")
         nc.sync.dma_start(out=q_raw[:], in_=query.rearrange("(p j) q -> p j q", j=PACK))
 
+        nc.sync.dma_start(oppo_list[:], offs3)
         k_scales = sb.tile([P, PLANE], U8, name="k_scales", align_bytes=64)
         nc.vector.memset(k_scales[:].bitcast(U32), 0)
         for quad in range(4):
-            nc.scalar.dma_start(
+            queue = nc.sync if quad % 2 == 0 else nc.scalar
+            queue.dma_start(
                 out=k_scales[32 * quad : 32 * quad + 16, :].bitcast(I32),
                 in_=keys_scales[0, 4 * quad : 4 * quad + 4, :]
                 .bitcast(I32)
@@ -64,7 +66,6 @@ def tile_attend_seconded_outside_moved_heads_kernel(
             )
             k_words.append(kw)
 
-        nc.sync.dma_start(oppo_list[:], offs3)
         nc.sync.dma_start(second_list[:], offs2)
         nc.sync.dma_start(own_list[:], offs)
         lam_t = sb.tile([P, 1], F32, name="lam_t")

@@ -11,7 +11,7 @@ KEY_LOAD = 512
 PLANE = 256
 PASSES = [256,256,256,128,128]
 FIRST = 128
-STORES = [128,256,256,256,128]
+STORES = [128,192,256,256,192]
 
 F32 = mybir.dt.float32
 BF16 = mybir.dt.bfloat16

from contextlib import ExitStack

import concourse.mybir as mybir

D, T, SLOTS, Q, RUN = 512, 1024, 512, 128, 8
P = 128
PACK = 4
HALF = SLOTS // 2
GROUPS = SLOTS // RUN
KEY_LOAD = 512
PLANE = 256
PASSES = [256,256,256,128,128]
FIRST = 128
STORES = [128,192,256,256,192]

F32 = mybir.dt.float32
BF16 = mybir.dt.bfloat16
I32 = mybir.dt.int32
U32 = mybir.dt.uint32
U16 = mybir.dt.uint16
U8 = mybir.dt.uint8
FP8X4 = mybir.dt.float8_e4m3fn_x4
ALU = mybir.AluOpType
ACT = mybir.ActivationFunctionType
AX = mybir.AxisListType

FLOPS = 2 * D * Q * T


def tile_attend_seconded_outside_moved_heads_kernel(
    tc, query, keys_words, keys_scales, lam, old, gainm, offs, offs2, offs3, offs4, out
):
    nc = tc.nc
    with ExitStack() as ctx:
        lists = ctx.enter_context(tc.tile_pool(name="lists", bufs=1))
        sb = ctx.enter_context(tc.tile_pool(name="sb", bufs=1))
        ps = ctx.enter_context(tc.psum_pool(name="ps", bufs=1))

        own_list = lists.tile([P, SLOTS // 16], U16, name="own_list")
        second_list = lists.tile([P, SLOTS // 16], U16, name="second_list")
        oppo_list = lists.tile([P, SLOTS // 16], U16, name="oppo_list")
        place_list = lists.tile([P, SLOTS // 16], U16, name="place_list")

        q_raw = sb.tile([P, PACK, Q], F32, name="q_raw")
        nc.sync.dma_start(out=q_raw[:], in_=query.rearrange("(p j) q -> p j q", j=PACK))

        nc.sync.dma_start(oppo_list[:], offs3)
        k_scales = sb.tile([P, PLANE], U8, name="k_scales", align_bytes=64)
        nc.vector.memset(k_scales[:].bitcast(U32), 0)
        for quad in range(4):
            queue = nc.sync if quad % 2 == 0 else nc.scalar
            queue.dma_start(
                out=k_scales[32 * quad : 32 * quad + 16, :].bitcast(I32),
                in_=keys_scales[0, 4 * quad : 4 * quad + 4, :]
                .bitcast(I32)
                .rearrange("r (v c) -> v r c", v=T // PLANE),
            )

        words = keys_words[0].rearrange("p n t -> p (n t)")
        k_words = []
        for b in range(T // KEY_LOAD):
            kw = sb.tile([P, KEY_LOAD], U32, name="k_words%d" % b, align_bytes=64)
            nc.sync.dma_start(
                out=kw[:].bitcast(I32),
                in_=words[:, b * KEY_LOAD * PACK : (b + 1) * KEY_LOAD * PACK].bitcast(I32),
            )
            k_words.append(kw)

        nc.sync.dma_start(second_list[:], offs2)
        nc.sync.dma_start(own_list[:], offs)
        lam_t = sb.tile([P, 1], F32, name="lam_t")
        nc.sync.dma_start(out=lam_t[:], in_=lam)
        gain_t = sb.tile([P, SLOTS], F32, name="gain_t")
        nc.sync.dma_start(out=gain_t[:], in_=gainm)
        nc.sync.dma_start(place_list[:], offs4)
        old_t = sb.tile([P, T], F32, name="old_t")
        nc.sync.dma_start(out=old_t[:], in_=old)

        placed = sb.tile([P, T], F32, name="placed")
        nc.vector.memset(placed[:], 0.0)

        q_bf = sb.tile([P, Q, PACK], BF16, name="q_bf", align_bytes=64)
        q_words = sb.tile([P, Q], U32, name="q_words", align_bytes=64)
        q_scales = sb.tile([P, Q], U8, name="q_scales", align_bytes=64)
        q_halves = [slice(0, Q // 2), slice(Q // 2, Q)]
        for cols in q_halves:
            nc.vector.tensor_copy(
                out=q_bf[:, cols, :].rearrange("p (c i) t -> p c t i", i=4),
                in_=q_raw[:, :, cols].rearrange("p t (c i) -> p c t i", i=4),
            )
        for cols in q_halves:
            nc.vector.quantize_mx(
                out=q_words[:, cols].bitcast(FP8X4),
                scales=q_scales[:, cols],
                in_=q_bf[:, cols, :].rearrange("p q t -> p (q t)"),
            )

        scores = sb.tile([P, T], F32, name="scores")
        lo = 0
        for b, width in enumerate(PASSES):
            acc = ps.tile([P, width], F32, name="acc%d" % b)
            cols = slice(lo, lo + width)
            load, start = divmod(lo, KEY_LOAD)
            plane, first = divmod(lo, PLANE)
            lo = lo + width
            nc.tensor.matmul_mx(
                out=acc[:],
                lhsT=q_words[:].bitcast(FP8X4),
                lhsT_scale=q_scales[:],
                rhs=k_words[load][:, start : start + width].bitcast(FP8X4),
                rhs_scale=k_scales[4 * plane : P, first : first + width],
                start=True,
                stop=True,
            )
            if b % 2 == 1:
                nc.vector.tensor_copy(out=scores[:, cols], in_=acc[:])
            else:
                nc.scalar.activation(out=scores[:, cols], in_=acc[:], func=ACT.Copy)

        halves = [slice(h * HALF, (h + 1) * HALF) for h in range(2)]
        list_halves = [slice(h * HALF // 16, (h + 1) * HALF // 16) for h in range(2)]
        run_halves = [slice(h * GROUPS // 2, (h + 1) * GROUPS // 2) for h in range(2)]

        own = sb.tile([P, SLOTS], F32, name="own")
        oppo = [sb.tile([P, HALF], F32, name="oppo%d" % h) for h in range(2)]
        diff = [sb.tile([P, HALF], F32, name="diff%d" % h) for h in range(2)]
        bend = [sb.tile([P, HALF], F32, name="bend%d" % h) for h in range(2)]
        s_t = [sb.tile([P, HALF], F32, name="s%d" % h) for h in range(2)]
        p_t = sb.tile([P, SLOTS], F32, name="p_t")
        z_t = [sb.tile([P, 1], F32, name="z%d" % h) for h in range(2)]
        pg = sb.tile([P, GROUPS], F32, name="pg")
        den = sb.tile([P, GROUPS], F32, name="den")
        inv = sb.tile([P, GROUPS], F32, name="inv")
        spread = sb.tile([P, SLOTS], F32, name="spread")
        gained = sb.tile([P, SLOTS], F32, name="gained")
        neg_max = sb.tile([P, 1], F32, name="neg_max")

        nc.vector.tensor_copy(out=oppo[0][:], in_=scores[:].indirect(oppo_list[:, list_halves[0]]))
        nc.scalar.activation(
            out=oppo[1][:], in_=scores[:].indirect(oppo_list[:, list_halves[1]]), func=ACT.Copy
        )
        nc.scalar.activation(out=own[:], in_=scores[:].indirect(own_list[:]), func=ACT.Copy)
        for h in range(2):
            nc.vector.tensor_tensor(
                out=diff[h][:],
                in0=scores[:].indirect(second_list[:, list_halves[h]]),
                in1=oppo[h][:],
                op=ALU.subtract,
            )
        for h in range(2):
            nc.scalar.activation(out=bend[h][:], in_=diff[h][:], func=ACT.Tanh)
        nc.vector.tensor_reduce(out=neg_max[:], in_=own[:], axis=AX.X, op=ALU.max, negate=True)
        for h in range(2):
            nc.vector.scalar_tensor_tensor(
                out=s_t[h][:],
                in0=bend[h][:],
                scalar=lam_t[:],
                in1=own[:, halves[h]],
                op0=ALU.mult,
                op1=ALU.add,
            )
        for h in range(2):
            nc.scalar.activation(
                out=p_t[:, halves[h]], in_=s_t[h][:], func=ACT.Exp, bias=neg_max[:], accum_out=z_t[h][:]
            )
        def run_sums(h):
            nc.vector.tensor_reduce(
                out=pg[:, run_halves[h]],
                in_=p_t[:, halves[h]].rearrange("p (g j) -> p g j", j=RUN),
                axis=AX.X,
                op=ALU.add,
            )

        def times_gain(lo, hi):
            nc.vector.tensor_tensor(
                out=gained[:, lo:hi], in0=p_t[:, lo:hi], in1=gain_t[:, lo:hi], op=ALU.mult
            )

        def invert(lo, hi):
            runs = slice(lo // RUN, hi // RUN)
            nc.vector.reciprocal(out=inv[:, runs], in_=den[:, runs])
            nc.scalar.activation(
                out=spread[:, lo:hi].rearrange("p (g j) -> p g j", j=RUN),
                in_=inv[:, runs].unsqueeze(2).to_broadcast([P, (hi - lo) // RUN, RUN]),
                func=ACT.Copy,
                scale=64.0,
            )

        def place(lo, hi):
            nc.vector.tensor_tensor(
                out=placed[:].indirect(place_list[:, lo // 16 : hi // 16]),
                in0=gained[:, lo:hi],
                in1=spread[:, lo:hi],
                op=ALU.mult,
            )

        def outside(h):
            nc.scalar.activation(
                out=den[:, run_halves[h]],
                in_=pg[:, run_halves[h]],
                func=ACT.Identity,
                scale=-1.0,
                bias=z_all[:],
            )

        z_all = sb.tile([P, 1], F32, name="z_all")
        nc.scalar.activation(out=z_all[:], in_=z_t[0][:], func=ACT.Identity, bias=z_t[1][:])
        run_sums(0)
        run_sums(1)
        outside(0)
        outside(1)
        times_gain(0, HALF)
        times_gain(HALF, SLOTS - FIRST)
        invert(0, FIRST)
        invert(FIRST, SLOTS)
        times_gain(SLOTS - FIRST, SLOTS)
        place(0, FIRST)
        place(FIRST, SLOTS)

        lo = 0
        for c, width in enumerate(STORES):
            cols = slice(lo, lo + width)
            res = sb.tile([P, width], F32, name="res%d" % c)
            nc.vector.tensor_tensor(out=res[:], in0=placed[:, cols], in1=old_t[:, cols], op=ALU.add)
            queue = nc.sync if c % 2 == 0 else nc.scalar
            queue.dma_start(out=out[:, cols], in_=res[:])
            lo = lo + width
